import numpy as np, ml_dtypes
CORES = [34,162,290,418,42,426]
N = 6
TOK, CAP, FF = 512, 112, 4
def entries(a): return a.T.reshape(-1)
def pack(v, P): return np.ascontiguousarray(np.asarray(v, np.int32).reshape(-1, P).T)
def lists(rng, how):
    E = rng.integers(0, N, (N, TOK))
    if how == "hot": E[:] = rng.integers(N)
    if how == "none": E = (int(rng.integers(N)) + 1 + rng.integers(0, N - 1, (N, TOK))) % N
    if how == "skew": E = np.where(rng.random((N, TOK)) < 0.7, rng.integers(0, N, (N, 1)), E)
    if how == "even": E = np.stack([rng.permutation(np.arange(TOK) % N) for r in range(N)])
    if how == "own": E = np.repeat(np.arange(N).reshape(N, 1), TOK, axis=1)
    return {"ex": np.stack([pack(E[r], 16) for r in range(N)]), "pos": np.stack([pack(p, 16) for p in np.stack([np.array([np.sum(E[r, :t] == E[r, t]) for t in range(TOK)]) for r in range(N)])])}
def setup_inputs(rng):
    return dict({"x": rng.standard_normal((N, 128, TOK), dtype=np.float32).astype(ml_dtypes.bfloat16), "w1": (rng.standard_normal((N, 128, FF * 128), dtype=np.float32) / 8).astype(ml_dtypes.bfloat16), "w2": (rng.standard_normal((N, 128, FF * 128), dtype=np.float32) / 16).astype(ml_dtypes.bfloat16)}, **lists(rng, "uniform"))
def setup_inputs_even(rng):
    d = setup_inputs(rng); d.update(lists(rng, "even"))
    for k in ("x",): d[k] = (d[k].astype(np.float32) * 1024.0).astype(d[k].dtype)
    return d
def setup_inputs_hot(rng):
    d = setup_inputs(rng); d.update(lists(rng, "hot"))
    for k in ("x",): d[k] = (d[k].astype(np.float32) * (1 / 1024.0)).astype(d[k].dtype)
    return d
def setup_inputs_none(rng):
    d = setup_inputs(rng); d.update(lists(rng, "none"))
    return d
def setup_inputs_own(rng):
    d = setup_inputs(rng); d.update(lists(rng, "own"))
    return d
def setup_inputs_skew(rng):
    d = setup_inputs(rng); d.update(lists(rng, "skew"))
    return d
def check_inputs(x):
    bad = []
    if x["ex"].min() < 0 or x["ex"].max() >= N: bad.append("ex out of range")
    E = np.stack([entries(a) for a in x["ex"]])
    if not np.array_equal(np.stack([entries(a) for a in x["pos"]]), np.stack([np.array([np.sum(E[r, :t] == E[r, t]) for t in range(TOK)]) for r in range(N)])): bad.append("pos isn't the place")
    return bad
def reference(x, w1, w2, ex, pos):
    X, W1, W2 = x.astype(np.float64), w1.astype(np.float64), w2.astype(np.float64)
    y = np.zeros((N, 128, TOK))
    for r in range(N):
        E = entries(ex[r]); place = np.array([np.sum(E[:t] == E[t]) for t in range(TOK)])
        for k in range(N):
            m = (E == k) & (place < CAP)
            y[r][:, m] = sum(W2[k][:, 128 * f:128 * f + 128].T @ np.maximum(W1[k][:, 128 * f:128 * f + 128].T @ X[r][:, m], 0.0) for f in range(FF))
    return {"y": y.astype(ml_dtypes.bfloat16)}

@@ -1,0 +1,225 @@
+from concourse.mybir import AluOpType, ActivationFunctionType
+
+N, TOK, CAP, FF, D = 6, 512, 112, 4, 128
+RST = CAP + 8
+HALF = 2 * CAP
+
+SCRATCH = {
+    "idx": ("sbuf", [128, 32], "int32"),
+    "idxf": ("sbuf", [128, 64], "float32"),
+    "rc": ("sbuf", [128, 128], "float32"),
+    "rm": ("sbuf", [128, 256], "float32"),
+    "off": ("sbuf", [128, 32], "uint16"),
+    "offg": ("sbuf", [128, 32], "uint16"),
+    "xsb": ("sbuf", [128, TOK], "bfloat16"),
+    "win": ("sbuf", [128, N * TOK], "bfloat16"),
+    "wsb": ("sbuf", [128, 2 * FF * D], "bfloat16"),
+    "tin": ("sbuf", [128, N * CAP], "bfloat16"),
+    "hsb": ("sbuf", [128, 2 * FF * CAP], "bfloat16"),
+    "rout": ("sbuf", [128, N * CAP], "bfloat16"),
+    "res": ("sbuf", [128, N * RST], "bfloat16"),
+    "ysb": ("sbuf", [128, TOK], "bfloat16"),
+    "pha": ("psum", [128, 512], "float32"),
+    "phb": ("psum", [128, 512], "float32"),
+    "pso": ("psum", [128, 512], "float32"),
+    "psi": ("psum", [128, 512], "float32"),
+    "psj": ("psum", [128, 512], "float32"),
+}
+SEMAPHORES = ["ms", "gs", "r2", "idxld", "xld", "wa1", "wa2", "zs", "v1", "v1b", "pi", "pj", "v2", "v2b", "sc",
+              "tok0", "tok1", "tok2", "tok3", "tok4", "tok5", "l1a", "l1b", "ra", "rb", "l2", "cp",
+              "resarr", "sent", "gat", "yst"]
+
+_CACHE = {}
+
+
+def _bits(m):
+    return bin(m).count("1")
+
+
+def _hops(topo, a, b):
+    if topo.host(a) == topo.host(b) and topo.chip(a) == topo.chip(b):
+        return 0
+    if topo.rack(topo.host(a)) == topo.rack(topo.host(b)):
+        return 1 if (topo.mates(a, b) or topo.same_plane(a, b)) else 2
+    twin = topo.host(b) * topo.CORES_PER_HOST + a % topo.CORES_PER_HOST
+    return 1 + _hops(topo, twin, b)
+
+
+def _plan(cores, topo):
+    if "p" in _CACHE:
+        return _CACHE["p"]
+    n = len(cores)
+    both = lambda a, b: topo.may_write(a, b) and topo.may_write(b, a)
+    far = {k: [s for s in range(n) if s != k and not both(cores[s], cores[k])] for k in range(n)}
+    world = (max(topo.host(c) for c in cores) + 1) * topo.CORES_PER_HOST
+    used, proxy = set(cores), {}
+    for k in range(n):
+        if not far[k]:
+            continue
+        e, best = cores[k], None
+        for c in range(world):
+            if c in used or not topo.may_write(e, c) or not all(both(cores[s], c) for s in far[k]):
+                continue
+            key = (_hops(topo, e, c),
+                   topo.rack(topo.host(e)) != topo.rack(topo.host(c)),
+                   topo.die(e) != topo.die(c),
+                   sum(_hops(topo, cores[s], c) + _hops(topo, c, cores[s]) for s in far[k]), c)
+            if best is None or key < best:
+                best = key
+        proxy[k] = best[-1]
+        used.add(proxy[k])
+    order = {s: [k for k in range(n) if s in far[k]] for s in range(n)}
+    left = {s: [k for k in range(n) if k != s and s not in far[k]] for s in range(n)}
+    turn = {}
+    for s in range(n):
+        for t, k in enumerate(order[s]):
+            turn[(s, k)] = t
+    t = 0
+    while any(left.values()):
+        busy = set()
+        todo = sorted((s for s in range(n) if left[s] and len(order[s]) <= t), key=lambda s: (-len(left[s]), s))
+        for s in todo:
+            inc = lambda k: sum(1 for q in range(n) if k in left[q])
+            free = sorted((k for k in left[s] if k not in busy), key=lambda k: (-inc(k), (k - s) % n))
+            if not free:
+                continue
+            k = free[0]
+            busy.add(k)
+            left[s].remove(k)
+            order[s].append(k)
+            turn[(s, k)] = t
+        t += 1
+    chunks = {}
+    for k in range(n):
+        near = sorted((s for s in range(n) if s != k and s not in far[k]), key=lambda s: (turn[(s, k)], s))
+        chunks[cores[k]] = (k, [k] + near)
+        if far[k]:
+            chunks[proxy[k]] = (k, sorted(far[k], key=lambda s: (turn[(s, k)], s)))
+    _CACHE["p"] = (far, proxy, order, chunks)
+    return _CACHE["p"]
+
+
+def rank_program(g, core, T, topo):
+    cores = list(T.cores)
+    far, proxy, order, chunks = _plan(cores, topo)
+    if core not in chunks:
+        return
+    rank = T.rank_of(core)
+    sem = T.sem
+    te, ve, se, sy = g.tensor, g.vector, g.scalar, g.sync
+    sent = [0]
+
+    def send(dst, out_ap, in_ap, rsem):
+        rid, pid = topo.addr(dst, core)
+        m = topo.mask(core, dst)
+        g.remote_dma(out_ap, in_ap, rsem, sem.sent, pid, rid, m)
+        sent[0] += _bits(m)
+
+    expert, sources = chunks[core]
+    W1, W2 = FF * D, 2 * FF * D
+
+    if rank is not None:
+        sy.dma_start(T.idx[0:16, :], T.ex[:, :]).then_inc(sem.idxld, 16)
+        se.dma_start(T.idx[16:32, :], T.pos[:, :]).then_inc(sem.idxld, 16)
+        sy.dma_start(T.wsb[:, 0:W1], T.w1[:, :]).then_inc(sem.wa1, 16)
+        sy.dma_start(T.xsb[:, :], T.x[:, :]).then_inc(sem.xld, 16)
+        sy.dma_start(T.wsb[:, W1:W2], T.w2[:, :]).then_inc(sem.wa2, 16)
+
+        ve.memset(T.rc[0:32, :], float(TOK)).then_inc(sem.ms, 1)
+        for e in range(N):
+            ve.memset(T.win[:, e * TOK:e * TOK + CAP], 0.0).then_inc(sem.zs, 1)
+            ve.memset(T.res[:, e * RST + CAP:(e + 1) * RST], 0.0).then_inc(sem.zs, 1)
+        pat = [[0, 8], [-1, 16]]
+        g.wait_ge(sem.ms, 1)
+        g.affine_select(T.rm[0:32, 0:128], T.rc[0:32, :], pat, AluOpType.is_equal, 0.0, 0, 1).then_inc(sem.gs, 1)
+        g.wait_ge(sem.gs, 1)
+        g.affine_select(T.rm[0:32, 0:128], T.rm[0:32, 0:128], pat, AluOpType.not_equal, 1.0, -16, 1).then_inc(sem.gs, 1)
+        ve.wait_ge(sem.gs, 2)
+        ve.tensor_scalar(T.rm[0:32, 128:256], T.rm[0:32, 0:128], float(RST), None, AluOpType.min).then_inc(sem.r2, 1)
+
+        ve.wait_ge(sem.idxld, 32)
+        ve.tensor_copy(T.idxf[0:32, 0:32], T.idx[0:32, :]).then_inc(sem.v1, 1)
+        ve.tensor_scalar(T.idxf[0:32, 32:64], T.idx[0:32, :], float(CAP), None, AluOpType.min).then_inc(sem.v1b, 1)
+        te.wait_ge(sem.gs, 2)
+        te.wait_ge(sem.v1, 1)
+        te.matmul(T.psi[:, 0:32], T.rm[0:32, 0:128], T.idxf[0:32, 0:32], True, True).then_inc(sem.pi, 1)
+        te.wait_ge(sem.r2, 1)
+        te.wait_ge(sem.v1b, 1)
+        te.matmul(T.psj[:, 0:32], T.rm[0:32, 128:256], T.idxf[0:32, 32:64], True, True).then_inc(sem.pj, 1)
+        ve.wait_ge(sem.pi, 1)
+        ve.tensor_copy(T.off[:, :], T.psi[:, 0:32]).then_inc(sem.v2, 1)
+        ve.wait_ge(sem.v2, 1)
+        ve.wait_ge(sem.zs, 2 * N)
+        ve.wait_ge(sem.xld, 16)
+        ve.tensor_copy(T.win[:, 0:N * TOK].indirect(T.off[:, 0:32]), T.xsb[:, :]).then_inc(sem.sc, 1)
+        ve.wait_ge(sem.pj, 1)
+        ve.tensor_copy(T.offg[:, :], T.psj[:, 0:32]).then_inc(sem.v2b, 1)
+
+        if rank in proxy:
+            g.wait_ge(sem.wa1, 16)
+            send(proxy[rank], T.wsb[:, 0:W1], T.wsb[:, 0:W1], sem.wa1)
+            g.wait_ge(sem.wa2, 16)
+            send(proxy[rank], T.wsb[:, W1:W2], T.wsb[:, W1:W2], sem.wa2)
+        g.wait_ge(sem.sc, 1)
+        for k in order[rank]:
+            dst = proxy[k] if rank in far[k] else cores[k]
+            send(dst, T.tin[:, rank * CAP:(rank + 1) * CAP], T.win[:, k * TOK:k * TOK + CAP], sem["tok%d" % rank])
+        wval = 16
+    else:
+        wval = _bits(topo.mask(cores[expert], core))
+
+    for i, s in enumerate(sources):
+        own = cores[s] == core
+        hb = (i % 2) * FF * CAP
+        if own:
+            rhs, out = T.win[:, expert * TOK:expert * TOK + CAP], T.res[:, expert * RST:expert * RST + CAP]
+            te.wait_ge(sem.sc, 1)
+        else:
+            rhs, out = T.tin[:, s * CAP:(s + 1) * CAP], T.rout[:, i * CAP:(i + 1) * CAP]
+            te.wait_ge(sem["tok%d" % s], _bits(topo.mask(cores[s], core)))
+        if i == 0:
+            te.wait_ge(sem.wa1, wval)
+        for f in range(FF):
+            bank, lsem = (T.pha, sem.l1a) if f < 2 else (T.phb, sem.l1b)
+            c0 = (f % 2) * CAP
+            te.matmul(bank[:, c0:c0 + CAP], T.wsb[:, f * D:(f + 1) * D], rhs, True, True).then_inc(lsem, 1)
+        ve.wait_ge(sem.l1a, 2 * (i + 1))
+        ve.tensor_scalar(T.hsb[:, hb:hb + HALF], T.pha[:, 0:HALF], 0.0, None, AluOpType.max).then_inc(sem.ra, 1)
+        se.wait_ge(sem.l1b, 2 * (i + 1))
+        if i >= 2:
+            se.wait_ge(sem.l2, 4 * (i - 1))
+        se.activation(T.hsb[:, hb + HALF:hb + 2 * HALF], T.phb[:, 0:HALF], ActivationFunctionType.Relu).then_inc(sem.rb, 1)
+        te.wait_ge(sem.ra, i + 1)
+        if i == 0:
+            te.wait_ge(sem.wa2, wval)
+        else:
+            te.wait_ge(sem.cp, i)
+        for f in range(FF):
+            if f == 2:
+                te.wait_ge(sem.rb, i + 1)
+            te.matmul(T.pso[:, 0:CAP], T.wsb[:, W1 + f * D:W1 + (f + 1) * D], T.hsb[:, hb + f * CAP:hb + (f + 1) * CAP],
+                      f == 0, f == FF - 1).then_inc(sem.l2, 1)
+        ve.wait_ge(sem.l2, 4 * (i + 1))
+        ve.tensor_copy(out, T.pso[:, 0:CAP]).then_inc(sem.cp, 1)
+        if not own:
+            g.wait_ge(sem.cp, i + 1)
+            send(cores[s], T.res[:, expert * RST:expert * RST + CAP], out, sem.resarr)
+
+    if rank is not None:
+        landed = 0
+        for k in range(N):
+            if k != rank:
+                landed += _bits(topo.mask(proxy[k] if rank in far[k] else cores[k], core))
+        for q in (ve, se):
+            q.wait_ge(sem.resarr, landed)
+            q.wait_ge(sem.cp, len(sources))
+            q.wait_ge(sem.v2b, 1)
+            q.wait_ge(sem.zs, 2 * N)
+        h = TOK // 2
+        ve.tensor_copy(T.ysb[:, 0:h], T.res[:, 0:N * RST].indirect(T.offg[:, 0:16])).then_inc(sem.gat, 1)
+        se.activation(T.ysb[:, h:TOK], T.res[:, 0:N * RST].indirect(T.offg[:, 16:32]),
+                      ActivationFunctionType.Copy).then_inc(sem.gat, 1)
+        sy.wait_ge(sem.gat, 2)
+        sy.dma_start(T.y[:, :], T.ysb[:, :]).then_inc(sem.yst, 16)
+        sy.wait_ge(sem.yst, 16)
+    g.wait_ge(sem.sent, sent[0])

@@ -49,6 +49,7 @@ def _plan(cores, topo):
     if "p" in _CACHE:
         return _CACHE["p"]
     n = len(cores)
+    share = n // 2
     both = lambda a, b: topo.may_write(a, b) and topo.may_write(b, a)
     far = {k: [s for s in range(n) if s != k and not both(cores[s], cores[k])] for k in range(n)}
     world = (max(topo.host(c) for c in cores) + 1) * topo.CORES_PER_HOST
@@ -60,13 +61,18 @@ def _plan(cores, topo):
         for c in range(world):
             if c in used or not topo.may_write(e, c) or not all(both(cores[s], c) for s in far[k]):
                 continue
+            way = lambda s: _hops(topo, cores[s], c) + _hops(topo, c, cores[s])
+            more = sorted((s for s in range(n) if s != k and s not in far[k] and both(cores[s], c)),
+                          key=lambda s: (way(s), s))[:max(0, share - len(far[k]))]
             key = (_hops(topo, e, c),
                    topo.rack(topo.host(e)) != topo.rack(topo.host(c)),
-                   topo.die(e) != topo.die(c),
-                   sum(_hops(topo, cores[s], c) + _hops(topo, c, cores[s]) for s in far[k]), c)
+                   -len(more),
+                   topo.die(e) == topo.die(c),
+                   sum(way(s) for s in far[k] + more), c, more)
             if best is None or key < best:
                 best = key
-        proxy[k] = best[-1]
+        proxy[k] = best[-2]
+        far[k] = far[k] + best[-1]
         used.add(proxy[k])
     order = {s: [k for k in range(n) if s in far[k]] for s in range(n)}
     left = {s: [k for k in range(n) if k != s and s not in far[k]] for s in range(n)}

from concourse.mybir import AluOpType, ActivationFunctionType

N, TOK, CAP, FF, D = 6, 512, 112, 4, 128
RST = CAP + 8
HALF = 2 * CAP

SCRATCH = {
    "idx": ("sbuf", [128, 32], "int32"),
    "idxf": ("sbuf", [128, 64], "float32"),
    "rc": ("sbuf", [128, 128], "float32"),
    "rm": ("sbuf", [128, 256], "float32"),
    "off": ("sbuf", [128, 32], "uint16"),
    "offg": ("sbuf", [128, 32], "uint16"),
    "xsb": ("sbuf", [128, TOK], "bfloat16"),
    "win": ("sbuf", [128, N * TOK], "bfloat16"),
    "wsb": ("sbuf", [128, 2 * FF * D], "bfloat16"),
    "tin": ("sbuf", [128, N * CAP], "bfloat16"),
    "hsb": ("sbuf", [128, 2 * FF * CAP], "bfloat16"),
    "rout": ("sbuf", [128, N * CAP], "bfloat16"),
    "res": ("sbuf", [128, N * RST], "bfloat16"),
    "ysb": ("sbuf", [128, TOK], "bfloat16"),
    "pha": ("psum", [128, 512], "float32"),
    "phb": ("psum", [128, 512], "float32"),
    "pso": ("psum", [128, 512], "float32"),
    "psi": ("psum", [128, 512], "float32"),
    "psj": ("psum", [128, 512], "float32"),
}
SEMAPHORES = ["ms", "gs", "r2", "idxld", "xld", "wa1", "wa2", "zs", "v1", "v1b", "pi", "pj", "v2", "v2b", "sc",
              "tok0", "tok1", "tok2", "tok3", "tok4", "tok5", "l1a", "l1b", "ra", "rb", "l2", "cp",
              "resarr", "sent", "gat", "yst"]

_CACHE = {}


def _bits(m):
    return bin(m).count("1")


def _hops(topo, a, b):
    if topo.host(a) == topo.host(b) and topo.chip(a) == topo.chip(b):
        return 0
    if topo.rack(topo.host(a)) == topo.rack(topo.host(b)):
        return 1 if (topo.mates(a, b) or topo.same_plane(a, b)) else 2
    twin = topo.host(b) * topo.CORES_PER_HOST + a % topo.CORES_PER_HOST
    return 1 + _hops(topo, twin, b)


def _plan(cores, topo):
    if "p" in _CACHE:
        return _CACHE["p"]
    n = len(cores)
    share = n // 2
    both = lambda a, b: topo.may_write(a, b) and topo.may_write(b, a)
    far = {k: [s for s in range(n) if s != k and not both(cores[s], cores[k])] for k in range(n)}
    world = (max(topo.host(c) for c in cores) + 1) * topo.CORES_PER_HOST
    used, proxy = set(cores), {}
    for k in range(n):
        if not far[k]:
            continue
        e, best = cores[k], None
        for c in range(world):
            if c in used or not topo.may_write(e, c) or not all(both(cores[s], c) for s in far[k]):
                continue
            way = lambda s: _hops(topo, cores[s], c) + _hops(topo, c, cores[s])
            more = sorted((s for s in range(n) if s != k and s not in far[k] and both(cores[s], c)),
                          key=lambda s: (way(s), s))[:max(0, share - len(far[k]))]
            key = (_hops(topo, e, c),
                   topo.rack(topo.host(e)) != topo.rack(topo.host(c)),
                   -len(more),
                   topo.die(e) == topo.die(c),
                   sum(way(s) for s in far[k] + more), c, more)
            if best is None or key < best:
                best = key
        proxy[k] = best[-2]
        far[k] = far[k] + best[-1]
        used.add(proxy[k])
    order = {s: [k for k in range(n) if s in far[k]] for s in range(n)}
    left = {s: [k for k in range(n) if k != s and s not in far[k]] for s in range(n)}
    turn = {}
    for s in range(n):
        for t, k in enumerate(order[s]):
            turn[(s, k)] = t
    t = 0
    while any(left.values()):
        busy = set()
        todo = sorted((s for s in range(n) if left[s] and len(order[s]) <= t), key=lambda s: (-len(left[s]), s))
        for s in todo:
            inc = lambda k: sum(1 for q in range(n) if k in left[q])
            free = sorted((k for k in left[s] if k not in busy), key=lambda k: (-inc(k), (k - s) % n))
            if not free:
                continue
            k = free[0]
            busy.add(k)
            left[s].remove(k)
            order[s].append(k)
            turn[(s, k)] = t
        t += 1
    chunks = {}
    for k in range(n):
        near = sorted((s for s in range(n) if s != k and s not in far[k]), key=lambda s: (turn[(s, k)], s))
        chunks[cores[k]] = (k, [k] + near)
        if far[k]:
            chunks[proxy[k]] = (k, sorted(far[k], key=lambda s: (turn[(s, k)], s)))
    _CACHE["p"] = (far, proxy, order, chunks)
    return _CACHE["p"]


def rank_program(g, core, T, topo):
    cores = list(T.cores)
    far, proxy, order, chunks = _plan(cores, topo)
    if core not in chunks:
        return
    rank = T.rank_of(core)
    sem = T.sem
    te, ve, se, sy = g.tensor, g.vector, g.scalar, g.sync
    sent = [0]

    def send(dst, out_ap, in_ap, rsem):
        rid, pid = topo.addr(dst, core)
        m = topo.mask(core, dst)
        g.remote_dma(out_ap, in_ap, rsem, sem.sent, pid, rid, m)
        sent[0] += _bits(m)

    expert, sources = chunks[core]
    W1, W2 = FF * D, 2 * FF * D

    if rank is not None:
        sy.dma_start(T.idx[0:16, :], T.ex[:, :]).then_inc(sem.idxld, 16)
        se.dma_start(T.idx[16:32, :], T.pos[:, :]).then_inc(sem.idxld, 16)
        sy.dma_start(T.wsb[:, 0:W1], T.w1[:, :]).then_inc(sem.wa1, 16)
        sy.dma_start(T.xsb[:, :], T.x[:, :]).then_inc(sem.xld, 16)
        sy.dma_start(T.wsb[:, W1:W2], T.w2[:, :]).then_inc(sem.wa2, 16)

        ve.memset(T.rc[0:32, :], float(TOK)).then_inc(sem.ms, 1)
        for e in range(N):
            ve.memset(T.win[:, e * TOK:e * TOK + CAP], 0.0).then_inc(sem.zs, 1)
            ve.memset(T.res[:, e * RST + CAP:(e + 1) * RST], 0.0).then_inc(sem.zs, 1)
        pat = [[0, 8], [-1, 16]]
        g.wait_ge(sem.ms, 1)
        g.affine_select(T.rm[0:32, 0:128], T.rc[0:32, :], pat, AluOpType.is_equal, 0.0, 0, 1).then_inc(sem.gs, 1)
        g.wait_ge(sem.gs, 1)
        g.affine_select(T.rm[0:32, 0:128], T.rm[0:32, 0:128], pat, AluOpType.not_equal, 1.0, -16, 1).then_inc(sem.gs, 1)
        ve.wait_ge(sem.gs, 2)
        ve.tensor_scalar(T.rm[0:32, 128:256], T.rm[0:32, 0:128], float(RST), None, AluOpType.min).then_inc(sem.r2, 1)

        ve.wait_ge(sem.idxld, 32)
        ve.tensor_copy(T.idxf[0:32, 0:32], T.idx[0:32, :]).then_inc(sem.v1, 1)
        ve.tensor_scalar(T.idxf[0:32, 32:64], T.idx[0:32, :], float(CAP), None, AluOpType.min).then_inc(sem.v1b, 1)
        te.wait_ge(sem.gs, 2)
        te.wait_ge(sem.v1, 1)
        te.matmul(T.psi[:, 0:32], T.rm[0:32, 0:128], T.idxf[0:32, 0:32], True, True).then_inc(sem.pi, 1)
        te.wait_ge(sem.r2, 1)
        te.wait_ge(sem.v1b, 1)
        te.matmul(T.psj[:, 0:32], T.rm[0:32, 128:256], T.idxf[0:32, 32:64], True, True).then_inc(sem.pj, 1)
        ve.wait_ge(sem.pi, 1)
        ve.tensor_copy(T.off[:, :], T.psi[:, 0:32]).then_inc(sem.v2, 1)
        ve.wait_ge(sem.v2, 1)
        ve.wait_ge(sem.zs, 2 * N)
        ve.wait_ge(sem.xld, 16)
        ve.tensor_copy(T.win[:, 0:N * TOK].indirect(T.off[:, 0:32]), T.xsb[:, :]).then_inc(sem.sc, 1)
        ve.wait_ge(sem.pj, 1)
        ve.tensor_copy(T.offg[:, :], T.psj[:, 0:32]).then_inc(sem.v2b, 1)

        if rank in proxy:
            g.wait_ge(sem.wa1, 16)
            send(proxy[rank], T.wsb[:, 0:W1], T.wsb[:, 0:W1], sem.wa1)
            g.wait_ge(sem.wa2, 16)
            send(proxy[rank], T.wsb[:, W1:W2], T.wsb[:, W1:W2], sem.wa2)
        g.wait_ge(sem.sc, 1)
        for k in order[rank]:
            dst = proxy[k] if rank in far[k] else cores[k]
            send(dst, T.tin[:, rank * CAP:(rank + 1) * CAP], T.win[:, k * TOK:k * TOK + CAP], sem["tok%d" % rank])
        wval = 16
    else:
        wval = _bits(topo.mask(cores[expert], core))

    for i, s in enumerate(sources):
        own = cores[s] == core
        hb = (i % 2) * FF * CAP
        if own:
            rhs, out = T.win[:, expert * TOK:expert * TOK + CAP], T.res[:, expert * RST:expert * RST + CAP]
            te.wait_ge(sem.sc, 1)
        else:
            rhs, out = T.tin[:, s * CAP:(s + 1) * CAP], T.rout[:, i * CAP:(i + 1) * CAP]
            te.wait_ge(sem["tok%d" % s], _bits(topo.mask(cores[s], core)))
        if i == 0:
            te.wait_ge(sem.wa1, wval)
        for f in range(FF):
            bank, lsem = (T.pha, sem.l1a) if f < 2 else (T.phb, sem.l1b)
            c0 = (f % 2) * CAP
            te.matmul(bank[:, c0:c0 + CAP], T.wsb[:, f * D:(f + 1) * D], rhs, True, True).then_inc(lsem, 1)
        ve.wait_ge(sem.l1a, 2 * (i + 1))
        ve.tensor_scalar(T.hsb[:, hb:hb + HALF], T.pha[:, 0:HALF], 0.0, None, AluOpType.max).then_inc(sem.ra, 1)
        se.wait_ge(sem.l1b, 2 * (i + 1))
        if i >= 2:
            se.wait_ge(sem.l2, 4 * (i - 1))
        se.activation(T.hsb[:, hb + HALF:hb + 2 * HALF], T.phb[:, 0:HALF], ActivationFunctionType.Relu).then_inc(sem.rb, 1)
        te.wait_ge(sem.ra, i + 1)
        if i == 0:
            te.wait_ge(sem.wa2, wval)
        else:
            te.wait_ge(sem.cp, i)
        for f in range(FF):
            if f == 2:
                te.wait_ge(sem.rb, i + 1)
            te.matmul(T.pso[:, 0:CAP], T.wsb[:, W1 + f * D:W1 + (f + 1) * D], T.hsb[:, hb + f * CAP:hb + (f + 1) * CAP],
                      f == 0, f == FF - 1).then_inc(sem.l2, 1)
        ve.wait_ge(sem.l2, 4 * (i + 1))
        ve.tensor_copy(out, T.pso[:, 0:CAP]).then_inc(sem.cp, 1)
        if not own:
            g.wait_ge(sem.cp, i + 1)
            send(cores[s], T.res[:, expert * RST:expert * RST + CAP], out, sem.resarr)

    if rank is not None:
        landed = 0
        for k in range(N):
            if k != rank:
                landed += _bits(topo.mask(proxy[k] if rank in far[k] else cores[k], core))
        for q in (ve, se):
            q.wait_ge(sem.resarr, landed)
            q.wait_ge(sem.cp, len(sources))
            q.wait_ge(sem.v2b, 1)
            q.wait_ge(sem.zs, 2 * N)
        h = TOK // 2
        ve.tensor_copy(T.ysb[:, 0:h], T.res[:, 0:N * RST].indirect(T.offg[:, 0:16])).then_inc(sem.gat, 1)
        se.activation(T.ysb[:, h:TOK], T.res[:, 0:N * RST].indirect(T.offg[:, 16:32]),
                      ActivationFunctionType.Copy).then_inc(sem.gat, 1)
        sy.wait_ge(sem.gat, 2)
        sy.dma_start(T.y[:, :], T.ysb[:, :]).then_inc(sem.yst, 16)
        sy.wait_ge(sem.yst, 16)
    g.wait_ge(sem.sent, sent[0])
